import numpy as np
import ml_dtypes


def mxq(x, axis, fmt="e4m3"):
    dtype, down = {"e4m3": (ml_dtypes.float8_e4m3fn, 7), "e5m2": (ml_dtypes.float8_e5m2, 14)}[fmt]
    v = np.moveaxis(np.asarray(x, np.float32).astype(ml_dtypes.bfloat16).astype(np.float64), axis, -1)
    blocks = v.reshape(v.shape[:-1] + (-1, 32))
    amax = np.abs(blocks).max(-1, keepdims=True)
    byte = np.maximum(np.where(amax > 0, np.frexp(amax)[1] - 1 + 127, 0) - down, 1)
    scale = np.exp2(byte - 127.0)
    codes = (blocks / scale).astype(np.float32).astype(dtype).astype(np.float64)
    return np.moveaxis((codes * scale).reshape(v.shape), -1, axis)


WIDE = False


def mx_kscale(k):
    if not WIDE:
        return np.ones(k)
    levels = np.array([10, -10, 5, -5, 0])
    if k % 512:
        return np.exp2(np.random.permutation(np.resize(levels, k // 32))).repeat(32)
    a = np.empty((k // 512, 16))
    for p in range(k // 512):
        a[p, :8] = np.random.permutation(np.resize(levels, 8))
        for g in range(8):
            far = levels[np.abs(levels - a[p, g]) >= 10]
            a[p, g + 8] = far[np.random.randint(len(far))]
    return np.exp2(a.ravel()).repeat(32)


def f64(x):
    return np.asarray(x).astype(np.float64)


def striped8(idx):
    return np.concatenate([v.reshape(-1, 16).T for v in idx]).astype(np.uint16)


def unstriped8(offs):
    return np.stack([offs[16 * g:16 * g + 16].T.reshape(-1) for g in range(8)]).astype(np.int64)


E2M1 = np.array([0.0, 0.5, 1.0, 1.5, 2.0, 3.0, 4.0, 6.0, -0.0, -0.5, -1.0, -1.5, -2.0, -3.0, -4.0, -6.0])


def pack_weight(w, fmt):
    k, n = w.shape
    w = f64(np.asarray(w, np.float32).astype(ml_dtypes.bfloat16)).reshape(k // 32, 32, n)
    amax = np.abs(w).max(1)
    if fmt == "e4m3":
        byte = np.frexp(amax)[1] - 1 + 127 - 7
    else:
        mant, ex = np.frexp(amax / 6.0)
        byte = np.where(mant > 0.5, ex, ex - 1) + 127
    byte = np.clip(np.where(amax > 0, byte, 1), 1, 254)
    scaled = (w * np.exp2(127.0 - byte)[:, None, :]).reshape(k, n).astype(np.float32)
    by_word = np.ascontiguousarray(scaled.reshape(k // 512, 128, 4, n).transpose(0, 1, 3, 2))
    if fmt == "e4m3":
        words = by_word.astype(ml_dtypes.float8_e4m3fn).view(np.uint8)
    else:
        c = by_word.astype(ml_dtypes.float4_e2m1fn).view(np.uint8) & 0xF
        words = (c[..., 0::2] | (c[..., 1::2] << 4)).reshape(k // 512, 128, 2 * n)
    return np.ascontiguousarray(words), np.ascontiguousarray(byte.astype(np.uint8).reshape(k // 512, 16, n))


def unpack_weight(words, scales, fmt):
    g, _, n = scales.shape
    words = np.ascontiguousarray(words).reshape(g, 128, n, -1)
    if fmt == "e4m3":
        vals = words.view(ml_dtypes.float8_e4m3fn).astype(np.float64)
    else:
        nib = np.empty((g, 128, n, 4), np.uint8)
        nib[..., 0::2] = words & 0xF
        nib[..., 1::2] = words >> 4
        vals = E2M1[nib]
    vals = vals * np.repeat(np.exp2(scales.astype(np.float64) - 127.0), 8, axis=1)[..., None]
    return vals.transpose(0, 1, 3, 2).reshape(g * 512, n)


K, M, T, S = 1536, 1024, 1024, 512


def setup_inputs():
    n = np.random.standard_normal
    s = mx_kscale(K)[:, None]
    p_w = pack_weight(n((K, M)) / np.sqrt(K) / s, "e2m1")
    return {
        "xT": (n((K, T)) * s).astype(np.float32),
        "w_words": p_w[0],
        "w_scales": p_w[1],
        "wgt": np.repeat(np.random.uniform(0.5, 2.0, (8, S)), 16, axis=0).astype(np.float32),
        "b": (0.3 * n(1024)).astype(np.float32),
        "wgo": np.repeat(np.random.uniform(0.5, 2.0, (8, S)), 16, axis=0).astype(np.float32),
        "offs": striped8(np.stack([np.random.permutation(T)[:S] for _ in range(8)])),
        "offs2": striped8(np.stack([np.random.permutation(T)[:S] for _ in range(8)])),
    }


def reference(xT, w_words, w_scales, wgt, b, wgo, offs, offs2):
    idx = unstriped8(offs)
    group = np.arange(K) % 512 // 64
    xg = f64(wgt)[np.arange(K) // 4 % 128] * f64(xT)[np.arange(K)[:, None], idx[group]]
    xT_ = mxq(xg, 0, "e4m3")
    w_ = unpack_weight(w_words, w_scales, "e2m1")
    y = w_.T @ xT_
    place = unstriped8(offs2)[np.arange(M) % 128 // 16]
    out = np.zeros((M, T))
    out[np.arange(M)[:, None], place] = f64(wgo)[np.arange(M) % 128] * (y + f64(b)[:, None])
    return out

@@ -1,0 +1,169 @@
+import concourse.mybir as mybir
+from concourse.masks import make_identity
+
+K, M, T, S = 1536, 1024, 1024, 512
+
+FLOPS = 2 * K * M * S
+
+F32 = mybir.dt.float32
+BF16 = mybir.dt.bfloat16
+I32 = mybir.dt.int32
+U32 = mybir.dt.uint32
+U16 = mybir.dt.uint16
+U8 = mybir.dt.uint8
+E4M3X4 = mybir.dt.float8_e4m3fn_x4
+E2M1X4 = mybir.dt.float4_e2m1fn_x4
+MULT = mybir.AluOpType.mult
+IDENTITY = mybir.ActivationFunctionType.Identity
+
+P = 128
+PACK = 4
+PASSES = K // (P * PACK)
+M_TILES = M // P
+HALF = S // 2
+HALF_LIST = HALF // 16
+GROUP_N = 128
+VECTOR_ZEROED = 3
+
+
+def tile_list_hboth_bias_kernel(tc, xT, w_words, w_scales, wgt, b, wgo, offs, offs2, out):
+    nc = tc.nc
+    with (
+        tc.tile_pool(name="lists", bufs=1) as lists,
+        tc.tile_pool(name="keep", bufs=1) as keep,
+        tc.tile_pool(name="work", bufs=2) as work,
+        tc.psum_pool(name="psum", bufs=1) as psum,
+    ):
+        gather_list = lists.tile([P, S // 16], U16, name="gather_list")
+        scatter_list = lists.tile([P, S // 16], U16, name="scatter_list")
+
+        weight = [keep.tile([P, HALF], F32, name=f"weight{h}") for h in range(2)]
+        planes = [keep.tile([P, T], F32, name=f"plane{n}") for n in range(PASSES * PACK)]
+        words = keep.tile([P, PASSES, 2 * M], U8, name="words", align_bytes=64)
+        scales = keep.tile([P, PASSES, M], U8, name="scales", align_bytes=64)
+        factor = keep.tile([P, S], F32, name="factor")
+        windows = [keep.tile([P, T], F32, name=f"window{m}") for m in range(M_TILES)]
+        bias_rows = keep.tile([P, P], F32, name="bias_rows")
+        identity = keep.tile([P, P], F32, name="identity")
+        bias = keep.tile([P, M_TILES], F32, name="bias")
+        codes = [keep.tile([P, S], U32, name=f"codes{a}", align_bytes=64) for a in range(PASSES)]
+        code_scales = [keep.tile([P, S], U8, name=f"code_scales{a}", align_bytes=64) for a in range(PASSES)]
+
+        nc.sync.dma_start(gather_list[:], offs)
+        for h in range(2):
+            nc.scalar.dma_start(weight[h][:], wgt[:, h * HALF : (h + 1) * HALF])
+        x_view = xT.rearrange("(a p i) t -> a i p t", p=P, i=PACK)
+        for a in range(PASSES):
+            for i in range(PACK):
+                nc.sync.dma_start(planes[a * PACK + i][:], x_view[a, i])
+        nc.sync.dma_start(words[:].bitcast(I32), w_words.bitcast(I32).rearrange("a p n -> p a n"))
+        nc.sync.dma_start(scatter_list[:], offs2)
+        nc.sync.dma_start(factor[:], wgo)
+
+        nc.vector.memset(scales[:].rearrange("p a n -> p (a n)").bitcast(I32), 0)
+        for m in range(VECTOR_ZEROED):
+            nc.vector.memset(windows[m][:], 0.0)
+
+        nc.gpsimd.memset(bias_rows[:], 0.0)
+        nc.gpsimd.dma_start(bias_rows[0:M_TILES, :], b.rearrange("(m p) -> m p", p=P))
+        scales_view = w_scales.bitcast(I32)
+        for q in range(4):
+            nc.gpsimd.dma_start(
+                scales[32 * q : 32 * q + 4, :, :].bitcast(I32),
+                scales_view[:, 4 * q : 4 * q + 4, :].rearrange("a r n -> r a n"),
+            )
+        make_identity(nc, identity[:])
+        for m in range(VECTOR_ZEROED, M_TILES):
+            nc.gpsimd.memset(windows[m][:], 0.0)
+
+        banks = [psum.tile([P, S], F32, name=f"bank{m}") for m in range(M_TILES)]
+        nc.tensor.transpose(banks[M_TILES - 1][:, 0:P], bias_rows[:], identity[:])
+        nc.scalar.copy(bias[:], banks[M_TILES - 1][:, 0:M_TILES])
+
+        def gather(a, i, h, picked):
+            nc.vector.tensor_tensor(
+                picked[:, i, :],
+                planes[a * PACK + i][:].indirect(gather_list[:, h * HALF_LIST : (h + 1) * HALF_LIST]),
+                weight[h][:],
+                MULT,
+            )
+
+        def interleave(picked, grouped, h):
+            nc.scalar.copy(
+                grouped[:, h * HALF : (h + 1) * HALF, :].rearrange("p (c j) i -> p c i j", j=4),
+                picked[:].rearrange("p i (c j) -> p c i j", j=4),
+            )
+
+        def quantize(a, grouped, c0, c1):
+            nc.vector.quantize_mx(
+                out=codes[a][:, c0:c1].bitcast(E4M3X4),
+                scales=code_scales[a][:, c0:c1],
+                in_=grouped[:, c0:c1, :].rearrange("p c i -> p (c i)"),
+            )
+
+        waiting = None
+        for a in range(PASSES - 1):
+            picked = [work.tile([P, PACK, HALF], F32, name=f"picked{h}") for h in range(2)]
+            grouped = work.tile([P, S, PACK], BF16, name="grouped", align_bytes=64)
+            for i in range(PACK):
+                for h in range(2):
+                    gather(a, i, h, picked[h])
+                if i == 2 and waiting is not None:
+                    quantize(a - 1, waiting, 0, S)
+            for h in range(2):
+                interleave(picked[h], grouped, h)
+            waiting = grouped
+
+        last = PASSES - 1
+        picked = [work.tile([P, PACK, HALF], F32, name=f"picked{h}") for h in range(2)]
+        grouped = work.tile([P, S, PACK], BF16, name="grouped", align_bytes=64)
+        for i in range(PACK):
+            gather(last, i, 0, picked[0])
+        quantize(last - 1, waiting, 0, S)
+        interleave(picked[0], grouped, 0)
+        gather(last, 0, 1, picked[1])
+        gather(last, 1, 1, picked[1])
+        quantize(last, grouped, 0, HALF)
+        gather(last, 2, 1, picked[1])
+        gather(last, 3, 1, picked[1])
+
+        sums = [[keep.tile([P, HALF], F32, name=f"sum{h}_{m}") for m in range(M_TILES)] for h in range(2)]
+
+        def multiply(m, h):
+            for c0 in range(h * HALF, (h + 1) * HALF, GROUP_N):
+                for a in range(PASSES):
+                    nc.tensor.matmul_mx(
+                        out=banks[m][:, c0 : c0 + GROUP_N],
+                        lhsT=words[:, a, 2 * P * m : 2 * P * (m + 1)].bitcast(E2M1X4),
+                        lhsT_scale=scales[:, a, P * m : P * (m + 1)],
+                        rhs=codes[a][:, c0 : c0 + GROUP_N].bitcast(E4M3X4),
+                        rhs_scale=code_scales[a][:, c0 : c0 + GROUP_N],
+                        start=(a == 0),
+                        stop=(a == PASSES - 1),
+                    )
+
+        def add_bias(m, h):
+            nc.scalar.activation(sums[h][m][:], banks[m][:, h * HALF : (h + 1) * HALF], IDENTITY, bias=bias[:, m : m + 1])
+
+        def scatter(m, h):
+            nc.vector.tensor_tensor(
+                windows[m][:].indirect(scatter_list[:, h * HALF_LIST : (h + 1) * HALF_LIST]),
+                sums[h][m][:],
+                factor[:, h * HALF : (h + 1) * HALF],
+                MULT,
+            )
+
+        for m in range(M_TILES):
+            multiply(m, 0)
+            add_bias(m, 0)
+            scatter(m, 0)
+            if m == 1:
+                interleave(picked[1], grouped, 1)
+            if m == 2:
+                quantize(last, grouped, HALF, S)
+
+        for m in range(M_TILES):
+            multiply(m, 1)
+            add_bias(m, 1)
+            scatter(m, 1)
+            nc.sync.dma_start(out[P * m : P * (m + 1), :], windows[m][:])

@@ -24,6 +24,7 @@ HALF = S // 2
 HALF_LIST = HALF // 16
 GROUP_N = 128
 VECTOR_ZEROED = 3
+EARLY_TILES = 2
 
 
 def tile_list_hboth_bias_kernel(tc, xT, w_words, w_scales, wgt, b, wgo, offs, offs2, out):
@@ -39,7 +40,8 @@ def tile_list_hboth_bias_kernel(tc, xT, w_words, w_scales, wgt, b, wgo, offs, of
 
         weight = [keep.tile([P, HALF], F32, name=f"weight{h}") for h in range(2)]
         planes = [keep.tile([P, T], F32, name=f"plane{n}") for n in range(PASSES * PACK)]
-        words = keep.tile([P, PASSES, 2 * M], U8, name="words", align_bytes=64)
+        early_words = keep.tile([P, PASSES, 2 * P * EARLY_TILES], U8, name="early_words", align_bytes=64)
+        late_words = keep.tile([P, PASSES, 2 * P * (M_TILES - EARLY_TILES)], U8, name="late_words", align_bytes=64)
         scales = keep.tile([P, PASSES, M], U8, name="scales", align_bytes=64)
         factor = keep.tile([P, S], F32, name="factor")
         windows = [keep.tile([P, T], F32, name=f"window{m}") for m in range(M_TILES)]
@@ -56,25 +58,27 @@ def tile_list_hboth_bias_kernel(tc, xT, w_words, w_scales, wgt, b, wgo, offs, of
         for a in range(PASSES):
             for i in range(PACK):
                 nc.sync.dma_start(planes[a * PACK + i][:], x_view[a, i])
-        nc.sync.dma_start(words[:].bitcast(I32), w_words.bitcast(I32).rearrange("a p n -> p a n"))
-        nc.sync.dma_start(scatter_list[:], offs2)
-        nc.sync.dma_start(factor[:], wgo)
-
         nc.vector.memset(scales[:].rearrange("p a n -> p (a n)").bitcast(I32), 0)
-        for m in range(VECTOR_ZEROED):
-            nc.vector.memset(windows[m][:], 0.0)
-
-        nc.gpsimd.memset(bias_rows[:], 0.0)
-        nc.gpsimd.dma_start(bias_rows[0:M_TILES, :], b.rearrange("(m p) -> m p", p=P))
         scales_view = w_scales.bitcast(I32)
         for q in range(4):
-            nc.gpsimd.dma_start(
+            nc.sync.dma_start(
                 scales[32 * q : 32 * q + 4, :, :].bitcast(I32),
                 scales_view[:, 4 * q : 4 * q + 4, :].rearrange("a r n -> r a n"),
             )
+        words_view = w_words.bitcast(I32).rearrange("a p n -> p a n")
+        nc.sync.dma_start(early_words[:].bitcast(I32), words_view[:, :, 0 : EARLY_TILES * P // 2])
+        nc.sync.dma_start(scatter_list[:], offs2)
+        nc.sync.dma_start(factor[:], wgo)
+        nc.sync.dma_start(late_words[:].bitcast(I32), words_view[:, :, EARLY_TILES * P // 2 : M // 2])
+
+        for m in range(VECTOR_ZEROED):
+            nc.vector.memset(windows[m][:].bitcast(I32), 0)
+
+        nc.gpsimd.memset(bias_rows[:], 0.0)
+        nc.gpsimd.dma_start(bias_rows[0:M_TILES, :], b.rearrange("(m p) -> m p", p=P))
         make_identity(nc, identity[:])
         for m in range(VECTOR_ZEROED, M_TILES):
-            nc.gpsimd.memset(windows[m][:], 0.0)
+            nc.gpsimd.memset(windows[m][:].bitcast(I32), 0)
 
         banks = [psum.tile([P, S], F32, name=f"bank{m}") for m in range(M_TILES)]
         nc.tensor.transpose(banks[M_TILES - 1][:, 0:P], bias_rows[:], identity[:])
@@ -117,33 +121,53 @@ def tile_list_hboth_bias_kernel(tc, xT, w_words, w_scales, wgt, b, wgo, offs, of
         last = PASSES - 1
         picked = [work.tile([P, PACK, HALF], F32, name=f"picked{h}") for h in range(2)]
         grouped = work.tile([P, S, PACK], BF16, name="grouped", align_bytes=64)
-        for i in range(PACK):
-            gather(last, i, 0, picked[0])
-        quantize(last - 1, waiting, 0, S)
-        interleave(picked[0], grouped, 0)
-        gather(last, 0, 1, picked[1])
-        gather(last, 1, 1, picked[1])
+        for i in range(PACK - 1):
+            for h in range(2):
+                gather(last, i, h, picked[h])
+            if i == 1:
+                quantize(last - 1, waiting, 0, S)
+        for c0 in range(0, HALF, GROUP_N):
+            nc.vector.tensor_tensor(
+                picked[0][:, PACK - 1, c0 : c0 + GROUP_N],
+                planes[-1][:].indirect(gather_list[:, c0 // 16 : (c0 + GROUP_N) // 16]),
+                weight[0][:, c0 : c0 + GROUP_N],
+                MULT,
+            )
+        for c0, copy in ((0, nc.scalar.copy), (GROUP_N, nc.vector.tensor_copy)):
+            copy(
+                grouped[:, c0 : c0 + GROUP_N, :].rearrange("p (c j) i -> p c i j", j=4),
+                picked[0][:, :, c0 : c0 + GROUP_N].rearrange("p i (c j) -> p c i j", j=4),
+            )
         quantize(last, grouped, 0, HALF)
-        gather(last, 2, 1, picked[1])
-        gather(last, 3, 1, picked[1])
+        gather(last, PACK - 1, 1, picked[1])
 
         sums = [[keep.tile([P, HALF], F32, name=f"sum{h}_{m}") for m in range(M_TILES)] for h in range(2)]
 
-        def multiply(m, h):
-            for c0 in range(h * HALF, (h + 1) * HALF, GROUP_N):
-                for a in range(PASSES):
-                    nc.tensor.matmul_mx(
-                        out=banks[m][:, c0 : c0 + GROUP_N],
-                        lhsT=words[:, a, 2 * P * m : 2 * P * (m + 1)].bitcast(E2M1X4),
-                        lhsT_scale=scales[:, a, P * m : P * (m + 1)],
-                        rhs=codes[a][:, c0 : c0 + GROUP_N].bitcast(E4M3X4),
-                        rhs_scale=code_scales[a][:, c0 : c0 + GROUP_N],
-                        start=(a == 0),
-                        stop=(a == PASSES - 1),
-                    )
+        def product(m, h, c):
+            slot = 2 * m + c
+            return banks[slot % M_TILES][:, h * HALF + GROUP_N * (slot // M_TILES) : h * HALF + GROUP_N * (slot // M_TILES + 1)]
 
-        def add_bias(m, h):
-            nc.scalar.activation(sums[h][m][:], banks[m][:, h * HALF : (h + 1) * HALF], IDENTITY, bias=bias[:, m : m + 1])
+        def multiply(m, h, c, passes):
+            c0 = h * HALF + c * GROUP_N
+            for a in passes:
+                if m < EARLY_TILES:
+                    lhsT = early_words[:, a, 2 * P * m : 2 * P * (m + 1)]
+                else:
+                    lhsT = late_words[:, a, 2 * P * (m - EARLY_TILES) : 2 * P * (m - EARLY_TILES + 1)]
+                nc.tensor.matmul_mx(
+                    out=product(m, h, c),
+                    lhsT=lhsT.bitcast(E2M1X4),
+                    lhsT_scale=scales[:, a, P * m : P * (m + 1)],
+                    rhs=codes[a][:, c0 : c0 + GROUP_N].bitcast(E4M3X4),
+                    rhs_scale=code_scales[a][:, c0 : c0 + GROUP_N],
+                    start=(a == 0),
+                    stop=(a == PASSES - 1),
+                )
+
+        def add_bias(m, h, c):
+            nc.scalar.activation(
+                sums[h][m][:, c * GROUP_N : (c + 1) * GROUP_N], product(m, h, c), IDENTITY, bias=bias[:, m : m + 1]
+            )
 
         def scatter(m, h):
             nc.vector.tensor_tensor(
@@ -153,17 +177,17 @@ def tile_list_hboth_bias_kernel(tc, xT, w_words, w_scales, wgt, b, wgo, offs, of
                 MULT,
             )
 
-        for m in range(M_TILES):
-            multiply(m, 0)
-            add_bias(m, 0)
-            scatter(m, 0)
-            if m == 1:
-                interleave(picked[1], grouped, 1)
-            if m == 2:
-                quantize(last, grouped, HALF, S)
-
-        for m in range(M_TILES):
-            multiply(m, 1)
-            add_bias(m, 1)
-            scatter(m, 1)
-            nc.sync.dma_start(out[P * m : P * (m + 1), :], windows[m][:])
+        for c in range(2):
+            multiply(0, 0, c, range(PASSES - 1))
+        for h in range(2):
+            for m in range(M_TILES):
+                for c in range(2):
+                    multiply(m, h, c, range(PASSES - 1, PASSES) if h == m == 0 else range(PASSES))
+                    add_bias(m, h, c)
+                scatter(m, h)
+                if h == 0 and m == 1:
+                    interleave(picked[1], grouped, 1)
+                if h == 0 and m == 2:
+                    quantize(last, grouped, HALF, S)
+                if h == 1:
+                    nc.sync.dma_start(out[P * m : P * (m + 1), :], windows[m][:])

import concourse.mybir as mybir
from concourse.masks import make_identity

K, M, T, S = 1536, 1024, 1024, 512

FLOPS = 2 * K * M * S

F32 = mybir.dt.float32
BF16 = mybir.dt.bfloat16
I32 = mybir.dt.int32
U32 = mybir.dt.uint32
U16 = mybir.dt.uint16
U8 = mybir.dt.uint8
E4M3X4 = mybir.dt.float8_e4m3fn_x4
E2M1X4 = mybir.dt.float4_e2m1fn_x4
MULT = mybir.AluOpType.mult
IDENTITY = mybir.ActivationFunctionType.Identity

P = 128
PACK = 4
PASSES = K // (P * PACK)
M_TILES = M // P
HALF = S // 2
HALF_LIST = HALF // 16
GROUP_N = 128
VECTOR_ZEROED = 3
EARLY_TILES = 2


def tile_list_hboth_bias_kernel(tc, xT, w_words, w_scales, wgt, b, wgo, offs, offs2, out):
    nc = tc.nc
    with (
        tc.tile_pool(name="lists", bufs=1) as lists,
        tc.tile_pool(name="keep", bufs=1) as keep,
        tc.tile_pool(name="work", bufs=2) as work,
        tc.psum_pool(name="psum", bufs=1) as psum,
    ):
        gather_list = lists.tile([P, S // 16], U16, name="gather_list")
        scatter_list = lists.tile([P, S // 16], U16, name="scatter_list")

        weight = [keep.tile([P, HALF], F32, name=f"weight{h}") for h in range(2)]
        planes = [keep.tile([P, T], F32, name=f"plane{n}") for n in range(PASSES * PACK)]
        early_words = keep.tile([P, PASSES, 2 * P * EARLY_TILES], U8, name="early_words", align_bytes=64)
        late_words = keep.tile([P, PASSES, 2 * P * (M_TILES - EARLY_TILES)], U8, name="late_words", align_bytes=64)
        scales = keep.tile([P, PASSES, M], U8, name="scales", align_bytes=64)
        factor = keep.tile([P, S], F32, name="factor")
        windows = [keep.tile([P, T], F32, name=f"window{m}") for m in range(M_TILES)]
        bias_rows = keep.tile([P, P], F32, name="bias_rows")
        identity = keep.tile([P, P], F32, name="identity")
        bias = keep.tile([P, M_TILES], F32, name="bias")
        codes = [keep.tile([P, S], U32, name=f"codes{a}", align_bytes=64) for a in range(PASSES)]
        code_scales = [keep.tile([P, S], U8, name=f"code_scales{a}", align_bytes=64) for a in range(PASSES)]

        nc.sync.dma_start(gather_list[:], offs)
        for h in range(2):
            nc.scalar.dma_start(weight[h][:], wgt[:, h * HALF : (h + 1) * HALF])
        x_view = xT.rearrange("(a p i) t -> a i p t", p=P, i=PACK)
        for a in range(PASSES):
            for i in range(PACK):
                nc.sync.dma_start(planes[a * PACK + i][:], x_view[a, i])
        nc.vector.memset(scales[:].rearrange("p a n -> p (a n)").bitcast(I32), 0)
        scales_view = w_scales.bitcast(I32)
        for q in range(4):
            nc.sync.dma_start(
                scales[32 * q : 32 * q + 4, :, :].bitcast(I32),
                scales_view[:, 4 * q : 4 * q + 4, :].rearrange("a r n -> r a n"),
            )
        words_view = w_words.bitcast(I32).rearrange("a p n -> p a n")
        nc.sync.dma_start(early_words[:].bitcast(I32), words_view[:, :, 0 : EARLY_TILES * P // 2])
        nc.sync.dma_start(scatter_list[:], offs2)
        nc.sync.dma_start(factor[:], wgo)
        nc.sync.dma_start(late_words[:].bitcast(I32), words_view[:, :, EARLY_TILES * P // 2 : M // 2])

        for m in range(VECTOR_ZEROED):
            nc.vector.memset(windows[m][:].bitcast(I32), 0)

        nc.gpsimd.memset(bias_rows[:], 0.0)
        nc.gpsimd.dma_start(bias_rows[0:M_TILES, :], b.rearrange("(m p) -> m p", p=P))
        make_identity(nc, identity[:])
        for m in range(VECTOR_ZEROED, M_TILES):
            nc.gpsimd.memset(windows[m][:].bitcast(I32), 0)

        banks = [psum.tile([P, S], F32, name=f"bank{m}") for m in range(M_TILES)]
        nc.tensor.transpose(banks[M_TILES - 1][:, 0:P], bias_rows[:], identity[:])
        nc.scalar.copy(bias[:], banks[M_TILES - 1][:, 0:M_TILES])

        def gather(a, i, h, picked):
            nc.vector.tensor_tensor(
                picked[:, i, :],
                planes[a * PACK + i][:].indirect(gather_list[:, h * HALF_LIST : (h + 1) * HALF_LIST]),
                weight[h][:],
                MULT,
            )

        def interleave(picked, grouped, h):
            nc.scalar.copy(
                grouped[:, h * HALF : (h + 1) * HALF, :].rearrange("p (c j) i -> p c i j", j=4),
                picked[:].rearrange("p i (c j) -> p c i j", j=4),
            )

        def quantize(a, grouped, c0, c1):
            nc.vector.quantize_mx(
                out=codes[a][:, c0:c1].bitcast(E4M3X4),
                scales=code_scales[a][:, c0:c1],
                in_=grouped[:, c0:c1, :].rearrange("p c i -> p (c i)"),
            )

        waiting = None
        for a in range(PASSES - 1):
            picked = [work.tile([P, PACK, HALF], F32, name=f"picked{h}") for h in range(2)]
            grouped = work.tile([P, S, PACK], BF16, name="grouped", align_bytes=64)
            for i in range(PACK):
                for h in range(2):
                    gather(a, i, h, picked[h])
                if i == 2 and waiting is not None:
                    quantize(a - 1, waiting, 0, S)
            for h in range(2):
                interleave(picked[h], grouped, h)
            waiting = grouped

        last = PASSES - 1
        picked = [work.tile([P, PACK, HALF], F32, name=f"picked{h}") for h in range(2)]
        grouped = work.tile([P, S, PACK], BF16, name="grouped", align_bytes=64)
        for i in range(PACK - 1):
            for h in range(2):
                gather(last, i, h, picked[h])
            if i == 1:
                quantize(last - 1, waiting, 0, S)
        for c0 in range(0, HALF, GROUP_N):
            nc.vector.tensor_tensor(
                picked[0][:, PACK - 1, c0 : c0 + GROUP_N],
                planes[-1][:].indirect(gather_list[:, c0 // 16 : (c0 + GROUP_N) // 16]),
                weight[0][:, c0 : c0 + GROUP_N],
                MULT,
            )
        for c0, copy in ((0, nc.scalar.copy), (GROUP_N, nc.vector.tensor_copy)):
            copy(
                grouped[:, c0 : c0 + GROUP_N, :].rearrange("p (c j) i -> p c i j", j=4),
                picked[0][:, :, c0 : c0 + GROUP_N].rearrange("p i (c j) -> p c i j", j=4),
            )
        quantize(last, grouped, 0, HALF)
        gather(last, PACK - 1, 1, picked[1])

        sums = [[keep.tile([P, HALF], F32, name=f"sum{h}_{m}") for m in range(M_TILES)] for h in range(2)]

        def product(m, h, c):
            slot = 2 * m + c
            return banks[slot % M_TILES][:, h * HALF + GROUP_N * (slot // M_TILES) : h * HALF + GROUP_N * (slot // M_TILES + 1)]

        def multiply(m, h, c, passes):
            c0 = h * HALF + c * GROUP_N
            for a in passes:
                if m < EARLY_TILES:
                    lhsT = early_words[:, a, 2 * P * m : 2 * P * (m + 1)]
                else:
                    lhsT = late_words[:, a, 2 * P * (m - EARLY_TILES) : 2 * P * (m - EARLY_TILES + 1)]
                nc.tensor.matmul_mx(
                    out=product(m, h, c),
                    lhsT=lhsT.bitcast(E2M1X4),
                    lhsT_scale=scales[:, a, P * m : P * (m + 1)],
                    rhs=codes[a][:, c0 : c0 + GROUP_N].bitcast(E4M3X4),
                    rhs_scale=code_scales[a][:, c0 : c0 + GROUP_N],
                    start=(a == 0),
                    stop=(a == PASSES - 1),
                )

        def add_bias(m, h, c):
            nc.scalar.activation(
                sums[h][m][:, c * GROUP_N : (c + 1) * GROUP_N], product(m, h, c), IDENTITY, bias=bias[:, m : m + 1]
            )

        def scatter(m, h):
            nc.vector.tensor_tensor(
                windows[m][:].indirect(scatter_list[:, h * HALF_LIST : (h + 1) * HALF_LIST]),
                sums[h][m][:],
                factor[:, h * HALF : (h + 1) * HALF],
                MULT,
            )

        for c in range(2):
            multiply(0, 0, c, range(PASSES - 1))
        for h in range(2):
            for m in range(M_TILES):
                for c in range(2):
                    multiply(m, h, c, range(PASSES - 1, PASSES) if h == m == 0 else range(PASSES))
                    add_bias(m, h, c)
                scatter(m, h)
                if h == 0 and m == 1:
                    interleave(picked[1], grouped, 1)
                if h == 0 and m == 2:
                    quantize(last, grouped, HALF, S)
                if h == 1:
                    nc.sync.dma_start(out[P * m : P * (m + 1), :], windows[m][:])
